import numpy as np
import ml_dtypes

BF16 = ml_dtypes.bfloat16


def bf(x):
    return np.asarray(x, np.float32).astype(BF16)


def f32(x):
    return np.asarray(x, np.float32)


def f64(x):
    return np.asarray(x).astype(np.float64)


def striped(idx):
    return np.concatenate([l.reshape(-1, 16).T for l in idx])


def rows(idx, k):
    return np.tile(np.repeat(idx, 16, axis=0), (k // (16 * 8), 1))


def look(tab, idx):
    return np.take_along_axis(f64(tab), rows(idx, len(tab)), axis=1)


K, S, V, N, M = 512, 2048, 1024, 1024, 128


def silu(v):
    return v / (1.0 + np.exp(-v))


def setup_inputs():
    return {"tab": f32(np.random.standard_normal((2, K, S))), "w": bf(np.random.standard_normal((K, M)) / np.sqrt(K)), "b": f32(0.5 * np.random.standard_normal((M, 1))), "offs": striped(np.stack([np.random.permutation(S)[:N] for _ in range(8)]))}


def reference(tab, w, b, offs):
    idx = np.stack([g.T.reshape(-1) for g in np.split(offs, 8)])
    x = silu(look(tab[0], idx)) * look(tab[1], idx)
    y = f64(w).T @ x
    return np.maximum(y + f64(b), 0.0)

@@ -1,0 +1,63 @@
+import concourse.mybir as mybir
+
+P = 128
+ROWS = 512
+PLACES = 2048
+N = 1024
+M = 128
+BLOCKS = ROWS // P
+PIECE = 512
+PIECES = N // PIECE
+LISTED = 16
+
+FLOPS = 2 * ROWS * M * N
+
+F32 = mybir.dt.float32
+BF16 = mybir.dt.bfloat16
+U16 = mybir.dt.uint16
+ADD = mybir.AluOpType.add
+MAX = mybir.AluOpType.max
+MULT = mybir.AluOpType.mult
+SILU = mybir.ActivationFunctionType.Silu
+
+
+def tile_lookup_glu_silu_relu_kernel(tc, tab, w, b, offs, out):
+    nc = tc.nc
+    with (
+        tc.tile_pool(name="held", bufs=1) as held,
+        tc.tile_pool(name="work", bufs=4) as work,
+        tc.psum_pool(name="psum", bufs=1) as psum,
+    ):
+        offsets = held.tile([P, N // LISTED], U16, name="offsets")
+        nc.sync.dma_start(offsets[:], offs)
+
+        weights = held.tile([P, BLOCKS, M], BF16, name="weights")
+        nc.scalar.dma_start(weights[:], w.rearrange("(k p) m -> p k m", p=P))
+        bias = held.tile([P, 1], F32, name="bias")
+        nc.scalar.dma_start(bias[:], b)
+
+        gates, values = [], []
+        for k in range(BLOCKS):
+            gate = held.tile([P, PLACES], F32, name=f"gate{k}")
+            nc.sync.dma_start(gate[:], tab[0, k * P : (k + 1) * P, :])
+            gates.append(gate)
+            value = held.tile([P, PLACES], F32, name=f"value{k}")
+            nc.sync.dma_start(value[:], tab[1, k * P : (k + 1) * P, :])
+            values.append(value)
+
+        banks = [psum.tile([P, PIECE], F32, name=f"bank{c}") for c in range(PIECES)]
+        for k in range(BLOCKS):
+            for c in range(PIECES):
+                piece = offsets[:, c * PIECE // LISTED : (c + 1) * PIECE // LISTED]
+                activated = work.tile([P, PIECE], F32, name="activated")
+                nc.scalar.activation(activated[:], gates[k][:].indirect(piece), SILU)
+                product = work.tile([P, PIECE], F32, name="product")
+                nc.vector.tensor_tensor(product[:], values[k][:].indirect(piece), activated[:], MULT)
+                x = work.tile([P, PIECE], BF16, name="x")
+                nc.scalar.copy(x[:], product[:])
+                nc.tensor.matmul(banks[c][:], weights[:, k, :], x[:], start=(k == 0), stop=(k == BLOCKS - 1))
+
+        for c in range(PIECES):
+            result = work.tile([P, PIECE], F32, name="result")
+            nc.vector.tensor_scalar(result[:], banks[c][:], bias[:], 0.0, ADD, MAX)
+            nc.sync.dma_start(out[:, c * PIECE : (c + 1) * PIECE], result[:])

@@ -8,6 +8,7 @@ M = 128
 BLOCKS = ROWS // P
 PIECE = 512
 PIECES = N // PIECE
+FINE = PIECE // 2
 LISTED = 16
 
 FLOPS = 2 * ROWS * M * N
@@ -15,9 +16,8 @@ FLOPS = 2 * ROWS * M * N
 F32 = mybir.dt.float32
 BF16 = mybir.dt.bfloat16
 U16 = mybir.dt.uint16
-ADD = mybir.AluOpType.add
-MAX = mybir.AluOpType.max
 MULT = mybir.AluOpType.mult
+RELU = mybir.ActivationFunctionType.Relu
 SILU = mybir.ActivationFunctionType.Silu
 
 
@@ -45,19 +45,32 @@ def tile_lookup_glu_silu_relu_kernel(tc, tab, w, b, offs, out):
             nc.sync.dma_start(value[:], tab[1, k * P : (k + 1) * P, :])
             values.append(value)
 
-        banks = [psum.tile([P, PIECE], F32, name=f"bank{c}") for c in range(PIECES)]
+        banks = [psum.tile([P, FINE], F32, name=f"bank{q}") for q in range(N // FINE)]
         for k in range(BLOCKS):
-            for c in range(PIECES):
-                piece = offsets[:, c * PIECE // LISTED : (c + 1) * PIECE // LISTED]
-                activated = work.tile([P, PIECE], F32, name="activated")
-                nc.scalar.activation(activated[:], gates[k][:].indirect(piece), SILU)
-                product = work.tile([P, PIECE], F32, name="product")
-                nc.vector.tensor_tensor(product[:], values[k][:].indirect(piece), activated[:], MULT)
-                x = work.tile([P, PIECE], BF16, name="x")
-                nc.scalar.copy(x[:], product[:])
-                nc.tensor.matmul(banks[c][:], weights[:, k, :], x[:], start=(k == 0), stop=(k == BLOCKS - 1))
+            last = k == BLOCKS - 1
+            activated = work.tile([P, N], F32, name="activated")
+            for a in range(0, N, PIECE):
+                piece = offsets[:, a // LISTED : (a + PIECE) // LISTED]
+                nc.scalar.activation(activated[:, a : a + PIECE], gates[k][:].indirect(piece), SILU)
 
-        for c in range(PIECES):
-            result = work.tile([P, PIECE], F32, name="result")
-            nc.vector.tensor_scalar(result[:], banks[c][:], bias[:], 0.0, ADD, MAX)
-            nc.sync.dma_start(out[:, c * PIECE : (c + 1) * PIECE], result[:])
+            product = work.tile([P, N], F32, name="product")
+            x = work.tile([P, N], BF16, name="x")
+            width = FINE if last else PIECE
+            for a in range(0, N, width):
+                piece = offsets[:, a // LISTED : (a + width) // LISTED]
+                nc.vector.tensor_tensor(
+                    product[:, a : a + width], values[k][:].indirect(piece), activated[:, a : a + width], MULT
+                )
+                if last:
+                    nc.scalar.copy(x[:, a : a + width], product[:, a : a + width])
+                else:
+                    nc.vector.tensor_copy(x[:, a : a + width], product[:, a : a + width])
+            for q, bank in enumerate(banks):
+                nc.tensor.matmul(
+                    bank[:], weights[:, k, :], x[:, q * FINE : (q + 1) * FINE], start=(k == 0), stop=last
+                )
+
+        for q, bank in enumerate(banks):
+            result = work.tile([P, FINE], F32, name="result")
+            nc.scalar.activation(result[:], bank[:], RELU, bias=bias[:])
+            nc.sync.dma_start(out[:, q * FINE : (q + 1) * FINE], result[:])

@@ -33,8 +33,6 @@ def tile_lookup_glu_silu_relu_kernel(tc, tab, w, b, offs, out):
 
         weights = held.tile([P, BLOCKS, M], BF16, name="weights")
         nc.scalar.dma_start(weights[:], w.rearrange("(k p) m -> p k m", p=P))
-        bias = held.tile([P, 1], F32, name="bias")
-        nc.scalar.dma_start(bias[:], b)
 
         gates, values = [], []
         for k in range(BLOCKS):
@@ -44,33 +42,41 @@ def tile_lookup_glu_silu_relu_kernel(tc, tab, w, b, offs, out):
             value = held.tile([P, PLACES], F32, name=f"value{k}")
             nc.sync.dma_start(value[:], tab[1, k * P : (k + 1) * P, :])
             values.append(value)
+        bias = held.tile([P, 1], F32, name="bias")
+        nc.sync.dma_start(bias[:], b)
 
         banks = [psum.tile([P, FINE], F32, name=f"bank{q}") for q in range(N // FINE)]
+
+        def look_up(k, a, width, activated, product):
+            piece = offsets[:, a // LISTED : (a + width) // LISTED]
+            span = slice(a, a + width)
+            nc.vector.tensor_tensor(product[:, span], values[k][:].indirect(piece), activated[:, span], MULT)
+
+        def finish(q):
+            result = work.tile([P, FINE], F32, name="result")
+            nc.scalar.activation(result[:], banks[q][:], RELU, bias=bias[:])
+            nc.sync.dma_start(out[:, q * FINE : (q + 1) * FINE], result[:])
+
         for k in range(BLOCKS):
-            last = k == BLOCKS - 1
             activated = work.tile([P, N], F32, name="activated")
             for a in range(0, N, PIECE):
                 piece = offsets[:, a // LISTED : (a + PIECE) // LISTED]
                 nc.scalar.activation(activated[:, a : a + PIECE], gates[k][:].indirect(piece), SILU)
-
             product = work.tile([P, N], F32, name="product")
             x = work.tile([P, N], BF16, name="x")
-            width = FINE if last else PIECE
-            for a in range(0, N, width):
-                piece = offsets[:, a // LISTED : (a + width) // LISTED]
-                nc.vector.tensor_tensor(
-                    product[:, a : a + width], values[k][:].indirect(piece), activated[:, a : a + width], MULT
-                )
-                if last:
-                    nc.scalar.copy(x[:, a : a + width], product[:, a : a + width])
-                else:
-                    nc.vector.tensor_copy(x[:, a : a + width], product[:, a : a + width])
-            for q, bank in enumerate(banks):
-                nc.tensor.matmul(
-                    bank[:], weights[:, k, :], x[:, q * FINE : (q + 1) * FINE], start=(k == 0), stop=last
-                )
 
-        for q, bank in enumerate(banks):
-            result = work.tile([P, FINE], F32, name="result")
-            nc.scalar.activation(result[:], bank[:], RELU, bias=bias[:])
-            nc.sync.dma_start(out[:, q * FINE : (q + 1) * FINE], result[:])
+            if k < BLOCKS - 1:
+                for a in range(0, N, PIECE):
+                    look_up(k, a, PIECE, activated, product)
+                    nc.vector.tensor_copy(x[:, a : a + PIECE], product[:, a : a + PIECE])
+                for q, bank in enumerate(banks):
+                    nc.tensor.matmul(bank[:], weights[:, k, :], x[:, q * FINE : (q + 1) * FINE], start=(k == 0), stop=False)
+            else:
+                for q, bank in enumerate(banks):
+                    span = slice(q * FINE, (q + 1) * FINE)
+                    look_up(k, q * FINE, FINE, activated, product)
+                    nc.scalar.copy(x[:, span], product[:, span])
+                    nc.tensor.matmul(bank[:], weights[:, k, :], x[:, span], start=False, stop=True)
+                    if q > 0:
+                        finish(q - 1)
+                finish(len(banks) - 1)

@@ -16,6 +16,8 @@ FLOPS = 2 * ROWS * M * N
 F32 = mybir.dt.float32
 BF16 = mybir.dt.bfloat16
 U16 = mybir.dt.uint16
+ADD = mybir.AluOpType.add
+MAX = mybir.AluOpType.max
 MULT = mybir.AluOpType.mult
 RELU = mybir.ActivationFunctionType.Relu
 SILU = mybir.ActivationFunctionType.Silu
@@ -54,7 +56,10 @@ def tile_lookup_glu_silu_relu_kernel(tc, tab, w, b, offs, out):
 
         def finish(q):
             result = work.tile([P, FINE], F32, name="result")
-            nc.scalar.activation(result[:], banks[q][:], RELU, bias=bias[:])
+            if q < len(banks) // 2:
+                nc.scalar.activation(result[:], banks[q][:], RELU, bias=bias[:])
+            else:
+                nc.vector.tensor_scalar(result[:], banks[q][:], bias[:], 0.0, ADD, MAX)
             nc.sync.dma_start(out[:, q * FINE : (q + 1) * FINE], result[:])
 
         for k in range(BLOCKS):
@@ -75,7 +80,10 @@ def tile_lookup_glu_silu_relu_kernel(tc, tab, w, b, offs, out):
                 for q, bank in enumerate(banks):
                     span = slice(q * FINE, (q + 1) * FINE)
                     look_up(k, q * FINE, FINE, activated, product)
-                    nc.scalar.copy(x[:, span], product[:, span])
+                    if q < len(banks) - 1:
+                        nc.scalar.copy(x[:, span], product[:, span])
+                    else:
+                        nc.vector.tensor_copy(x[:, span], product[:, span])
                     nc.tensor.matmul(bank[:], weights[:, k, :], x[:, span], start=False, stop=True)
                     if q > 0:
                         finish(q - 1)

@@ -34,8 +34,6 @@ def tile_lookup_glu_silu_relu_kernel(tc, tab, w, b, offs, out):
         nc.sync.dma_start(offsets[:], offs)
 
         weights = held.tile([P, BLOCKS, M], BF16, name="weights")
-        nc.scalar.dma_start(weights[:], w.rearrange("(k p) m -> p k m", p=P))
-
         gates, values = [], []
         for k in range(BLOCKS):
             gate = held.tile([P, PLACES], F32, name=f"gate{k}")
@@ -44,6 +42,8 @@ def tile_lookup_glu_silu_relu_kernel(tc, tab, w, b, offs, out):
             value = held.tile([P, PLACES], F32, name=f"value{k}")
             nc.sync.dma_start(value[:], tab[1, k * P : (k + 1) * P, :])
             values.append(value)
+            if k == 0:
+                nc.sync.dma_start(weights[:], w.rearrange("(k p) m -> p k m", p=P))
         bias = held.tile([P, 1], F32, name="bias")
         nc.sync.dma_start(bias[:], b)
 

import concourse.mybir as mybir

P = 128
ROWS = 512
PLACES = 2048
N = 1024
M = 128
BLOCKS = ROWS // P
PIECE = 512
PIECES = N // PIECE
FINE = PIECE // 2
LISTED = 16

FLOPS = 2 * ROWS * M * N

F32 = mybir.dt.float32
BF16 = mybir.dt.bfloat16
U16 = mybir.dt.uint16
ADD = mybir.AluOpType.add
MAX = mybir.AluOpType.max
MULT = mybir.AluOpType.mult
RELU = mybir.ActivationFunctionType.Relu
SILU = mybir.ActivationFunctionType.Silu


def tile_lookup_glu_silu_relu_kernel(tc, tab, w, b, offs, out):
    nc = tc.nc
    with (
        tc.tile_pool(name="held", bufs=1) as held,
        tc.tile_pool(name="work", bufs=4) as work,
        tc.psum_pool(name="psum", bufs=1) as psum,
    ):
        offsets = held.tile([P, N // LISTED], U16, name="offsets")
        nc.sync.dma_start(offsets[:], offs)

        weights = held.tile([P, BLOCKS, M], BF16, name="weights")
        gates, values = [], []
        for k in range(BLOCKS):
            gate = held.tile([P, PLACES], F32, name=f"gate{k}")
            nc.sync.dma_start(gate[:], tab[0, k * P : (k + 1) * P, :])
            gates.append(gate)
            value = held.tile([P, PLACES], F32, name=f"value{k}")
            nc.sync.dma_start(value[:], tab[1, k * P : (k + 1) * P, :])
            values.append(value)
            if k == 0:
                nc.sync.dma_start(weights[:], w.rearrange("(k p) m -> p k m", p=P))
        bias = held.tile([P, 1], F32, name="bias")
        nc.sync.dma_start(bias[:], b)

        banks = [psum.tile([P, FINE], F32, name=f"bank{q}") for q in range(N // FINE)]

        def look_up(k, a, width, activated, product):
            piece = offsets[:, a // LISTED : (a + width) // LISTED]
            span = slice(a, a + width)
            nc.vector.tensor_tensor(product[:, span], values[k][:].indirect(piece), activated[:, span], MULT)

        def finish(q):
            result = work.tile([P, FINE], F32, name="result")
            if q < len(banks) // 2:
                nc.scalar.activation(result[:], banks[q][:], RELU, bias=bias[:])
            else:
                nc.vector.tensor_scalar(result[:], banks[q][:], bias[:], 0.0, ADD, MAX)
            nc.sync.dma_start(out[:, q * FINE : (q + 1) * FINE], result[:])

        for k in range(BLOCKS):
            activated = work.tile([P, N], F32, name="activated")
            for a in range(0, N, PIECE):
                piece = offsets[:, a // LISTED : (a + PIECE) // LISTED]
                nc.scalar.activation(activated[:, a : a + PIECE], gates[k][:].indirect(piece), SILU)
            product = work.tile([P, N], F32, name="product")
            x = work.tile([P, N], BF16, name="x")

            if k < BLOCKS - 1:
                for a in range(0, N, PIECE):
                    look_up(k, a, PIECE, activated, product)
                    nc.vector.tensor_copy(x[:, a : a + PIECE], product[:, a : a + PIECE])
                for q, bank in enumerate(banks):
                    nc.tensor.matmul(bank[:], weights[:, k, :], x[:, q * FINE : (q + 1) * FINE], start=(k == 0), stop=False)
            else:
                for q, bank in enumerate(banks):
                    span = slice(q * FINE, (q + 1) * FINE)
                    look_up(k, q * FINE, FINE, activated, product)
                    if q < len(banks) - 1:
                        nc.scalar.copy(x[:, span], product[:, span])
                    else:
                        nc.vector.tensor_copy(x[:, span], product[:, span])
                    nc.tensor.matmul(bank[:], weights[:, k, :], x[:, span], start=False, stop=True)
                    if q > 0:
                        finish(q - 1)
                finish(len(banks) - 1)
